import numpy as np, ml_dtypes
CORES = [8,11,14,16,19,22,24,27,30]
N = 9
import mx_ref
NC = 128
BF = ml_dtypes.bfloat16
def setup_inputs(rng):
    def f(*shape):
        return mx_ref.flush((rng.standard_normal(shape, dtype=np.float32) * np.exp2(rng.integers(-2, 3, shape[:-1] + (1,)))).astype(BF))
    return {"w": f(N, 128, N * 512), "x": f(N, 128, N * 4 * NC)}
def setup_inputs_blocks(rng):
    d = setup_inputs(rng)
    for k in ("w", "x"): d[k] = mx_ref.spread(d[k], rng, 2)
    return d
def setup_inputs_wide(rng):
    d = setup_inputs(rng)
    for k in ("w", "x"): d[k] = mx_ref.flush((d[k].astype(np.float32) * np.exp2(rng.integers(-8, 9, (N, 1, 1))).astype(np.float32)).astype(BF))
    return d
def setup_inputs_zeros(rng):
    d = setup_inputs(rng); v = d["x"].reshape(N, 128, -1, 4).copy()
    v[np.broadcast_to((rng.random((N, 1, v.shape[2], 1)) < 0.33), v.shape)] = 0
    d["x"] = v.reshape(d["x"].shape)
    return d
def reference(w, x):
    y = np.zeros((N, 128, NC), np.float32)
    for r in range(N):
        for j in range(N):
            p = mx_ref.matmul(mx_ref.quantize(w[r][:, 512 * j:512 * j + 512]), mx_ref.quantize(x[j][:, 4 * NC * r:4 * NC * r + 4 * NC]))
            y[r] = p if j == 0 else y[r] + p
    return {"y": y}

@@ -1,0 +1,287 @@
+from concourse.bass import DstId, RemoteDMATransfer
+from concourse.mybir import dt
+
+N = 9
+SIM_CORES = 32
+TW = 128
+TB = 4 * TW
+RELAY_TILES = 6
+W_FREE = 1
+HAND = False
+NEEDY_FIRST = True
+ABROAD = True
+PAIR = "direct"
+
+SCRATCH = {
+    "xb": ("sbuf", [128, N * TB], "bfloat16"),
+    "wb": ("sbuf", [128, N * TB], "bfloat16"),
+    "xq": ("sbuf", [128, N * TW], "float8_e4m3fn_x4"),
+    "xs": ("sbuf", [128, N * TW], "uint8"),
+    "wq": ("sbuf", [128, N * TW], "float8_e4m3fn_x4"),
+    "ws": ("sbuf", [128, N * TW], "uint8"),
+    "lq": ("sbuf", [128, N * TW], "float8_e4m3fn_x4"),
+    "ls": ("sbuf", [128, N * TW], "uint8"),
+    "rq": ("sbuf", [128, RELAY_TILES * TW], "float8_e4m3fn_x4"),
+    "rs": ("sbuf", [128, RELAY_TILES * TW], "uint8"),
+    "acc": ("psum", [128, 512], "float32"),
+    "yo": ("sbuf", [128, TW], "float32"),
+}
+SEMAPHORES = (["xl%d" % k for k in range(3)] + ["xd%d" % k for k in range(4)] + ["xo"]
+              + ["wl%d" % k for k in range(5)] + ["wd%d" % k for k in range(5)]
+              + ["a%d" % j for j in range(N)]
+              + ["bc%d" % k for k in range(3)] + ["bs%d" % k for k in range(3)]
+              + ["sent", "gate", "mm", "cp", "st"])
+
+
+def _bits(m):
+    return [e for e in range(m.bit_length()) if (m >> e) & 1]
+
+
+def _mask(es):
+    m = 0
+    for e in es:
+        m |= 1 << e
+    return m
+
+
+def _split(es, k, flip):
+    h = len(es) // 2
+    q = h // 2
+    if k == 1:
+        return [es]
+    if k == 2:
+        return [es[:h], es[h:]]
+    if flip:
+        return [es[:q], es[q:h], es[h:]]
+    return [es[:h], es[h:h + q], es[h + q:]]
+
+
+def _runs(ts):
+    out = []
+    for t in ts:
+        if out and out[-1][0] + out[-1][1] == t:
+            out[-1] = (out[-1][0], out[-1][1] + 1)
+        else:
+            out.append((t, 1))
+    return out
+
+
+def _plan(cores, topo):
+    n = len(cores)
+    chip = [topo.chip(c) for c in cores]
+    group = {}
+    for r in range(n):
+        group.setdefault(chip[r], []).append(r)
+    free = [c for c in range(SIM_CORES) if c not in cores]
+
+    def ok(c, rs):
+        return all(topo.may_write(c, cores[r]) for r in rs)
+
+    def hops(ca, cb):
+        return 0 if ca == cb else 1 if topo.mates(ca, cb) or topo.same_plane(ca, cb) else 2
+
+    busy = {}
+
+    def pick(s, cb):
+        cand = [c for c in free if topo.may_write(s, c) and ok(c, group[cb])]
+        h = min(cand, key=lambda c: (busy.get(c, 0), hops(topo.chip(s), topo.chip(c)) + hops(topo.chip(c), cb),
+                                     topo.chip(c) != topo.chip(s), topo.die(c) != topo.die(s),
+                                     sum(topo.may_write(c, o) for o in cores), c))
+        busy[h] = busy.get(h, 0) + 1
+        return h
+
+    reach = {j: [cb for cb in sorted(group) if cb != chip[j] and ok(cores[j], group[cb])] for j in range(n)}
+    ships = {}
+    for j in sorted(range(n), key=lambda j: (len(reach[j]) if NEEDY_FIRST or reach[j] else n, j)):
+        s = cores[j]
+        away = [cb for cb in sorted(group) if cb != chip[j]]
+        handed = [cb for cb in away if cb not in reach[j]]
+        if HAND and not handed:
+            idle = {cb: [c for c in free if topo.may_write(s, c) and not busy.get(c) and ok(c, group[cb])
+                         and (ABROAD or topo.chip(c) == chip[j])] for cb in away}
+            way = {cb: min([(hops(chip[j], topo.chip(c)) + hops(topo.chip(c), cb)) for c in idle[cb]] + [n])
+                   for cb in away}
+            best = min(away, key=lambda cb: (way[cb], -len(idle[cb])))
+            if idle[best]:
+                handed = [best]
+        mine = []
+        for cb in sorted(handed, key=lambda cb: -hops(chip[j], cb)):
+            mine.append({"tiles": list(group[cb]), "via": pick(s, cb)})
+        pair = [r for r in group[chip[j]] if r != j]
+        near = [sh for sh in mine if topo.chip(sh["via"]) == chip[j]]
+        if PAIR == "joined" and near:
+            near[-1]["tiles"] += pair
+            pair = []
+        for cb in sorted([cb for cb in away if cb not in handed], key=lambda cb: -hops(chip[j], cb)):
+            mine.append({"tiles": list(group[cb]), "via": None})
+        if pair:
+            mine.append({"tiles": pair, "via": near[-1]["via"] if PAIR == "helper" and near else None})
+        ships[j] = mine
+
+    pos = {}
+    for j in range(n):
+        seq = [r for sh in ships[j] for r in sh["tiles"]] + [j]
+        pos[j] = {r: i for i, r in enumerate(seq)}
+
+    calls, arrive, turn, slots, tasks, took = {}, {}, {}, {}, {}, {}
+
+    def lanes(c):
+        far = _bits(topo.mask(c, [o for o in cores if topo.chip(o) != topo.chip(c)][0]))
+        near = [e for e in _bits(topo.mask(c, [o for o in range(SIM_CORES) if topo.chip(o) == topo.chip(c) and o != c][0]))
+                if e not in far]
+        return far, near
+
+    def fan_out(c, waits, buf, where, j, tiles):
+        far, near = lanes(c)
+        out = [r for r in tiles if chip[r] != topo.chip(c)]
+        stay = [r for r in tiles if chip[r] == topo.chip(c)]
+        for part in ("c", "s"):
+            t = turn.get(c, 0)
+            share = dict(zip(out, _split(far, len(out), t % 4 in (1, 2)))) if out else {}
+            if out:
+                turn[c] = t + 1
+            if stay:
+                share.update(zip(stay, _split(near, len(stay), False)))
+            trs = []
+            for r in tiles:
+                trs.append((cores[r], buf, where[r], "l", j, 1, share[r], "a%d" % j))
+                arrive[(j, r)] = arrive.get((j, r), 0) + len(share[r])
+            calls.setdefault(c, []).append((waits[part], part, trs))
+
+    for k in range(max(len(s) for s in ships.values())):
+        for j in range(n):
+            if k >= len(ships[j]):
+                continue
+            sh, s = ships[j][k], cores[j]
+            ready = [("xd%d" % k, len(_runs(sh["tiles"])))]
+            if sh["via"] is None:
+                fan_out(s, {"c": ready, "s": []}, "x", pos[j], j, sh["tiles"])
+                continue
+            h = sh["via"]
+            far, near = lanes(s)
+            es = far
+            if topo.chip(h) == chip[j]:
+                must = sum(1 for o in ships[j] if (o["via"] is None and chip[o["tiles"][0]] != chip[j])
+                           or (o["via"] is not None and topo.chip(o["via"]) != chip[j]))
+                es = near if must or took.get(s) else far
+                took[s] = True
+            slot, t = slots.get(h, 0), tasks.get(h, 0)
+            slots[h], tasks[h] = slot + len(sh["tiles"]), t + 1
+            for part in ("c", "s"):
+                calls.setdefault(s, []).append((ready if part == "c" else [], part, [
+                    (h, "x", pos[j][sh["tiles"][0]], "r", slot, len(sh["tiles"]), es, "b%s%d" % (part, t))]))
+            fan_out(h, {"c": [("bc%d" % t, len(es))], "s": [("bs%d" % t, len(es))]}, "r",
+                    {r: slot + i for i, r in enumerate(sh["tiles"])}, j, sh["tiles"])
+
+    mm, wp = {}, {}
+    for r in range(n):
+        eta = {r: -1.0}
+        for j in range(n):
+            for k, sh in enumerate(ships[j]):
+                if r in sh["tiles"]:
+                    eta[j] = k + 1.5 * (sh["via"] is not None)
+        chips_in = sorted(group, key=lambda cb: max(eta[j] for j in group[cb]))
+        parts = []
+        for i, cb in enumerate(chips_in):
+            js = sorted(group[cb], key=lambda j: eta[j])
+            parts += [js[:-1], js[-1:]] if i == len(chips_in) - 1 else [js]
+        order, wparts = [], []
+        for js in parts:
+            for (t0, nt) in _runs(sorted(js)):
+                wparts.append((t0, nt))
+                order += [j for j in js if t0 <= j < t0 + nt]
+        mm[r], wp[r] = order, wparts
+    return {"ships": ships, "pos": pos, "calls": calls, "arrive": arrive, "mm": mm, "wp": wp, "group": group,
+            "chip": chip}
+
+
+def rank_program(g, core, T, topo):
+    cores = list(T.cores)
+    plan = _plan(cores, topo)
+    sem = T.sem
+    rank = T.rank_of(core)
+    codes = {"x": T.xq, "r": T.rq, "l": T.lq}
+    planes = {"x": T.xs, "r": T.rs, "l": T.ls}
+
+    def view(part, buf, tile, nt):
+        if part == "c":
+            return codes[buf][:, tile * TW:(tile + nt) * TW].bitcast(dt.uint8)
+        return planes[buf][:, tile * TW:(tile + nt) * TW]
+
+    if rank is not None:
+        ships, pos, group, chip = plan["ships"][rank], plan["pos"][rank], plan["group"], plan["chip"]
+        xchips = []
+        for r in [r for sh in ships for r in sh["tiles"]] + [rank]:
+            if chip[r] not in xchips:
+                xchips.append(chip[r])
+        for k, cb in enumerate(xchips):
+            a, b = group[cb][0] * TB, (group[cb][-1] + 1) * TB
+            q = g.sync if k % 2 == 0 else g.scalar
+            q.dma_start(T.xb[:, a:b], T.x[:, a:b]).then_inc(sem["xl%d" % k], 16)
+        wp = plan["wp"][rank]
+        for k, (t0, nt) in enumerate(wp):
+            if k == W_FREE:
+                g.scalar.wait_ge(sem.gate, 1)
+            g.scalar.dma_start(T.wb[:, t0 * TB:(t0 + nt) * TB],
+                               T.w[:, t0 * TB:(t0 + nt) * TB]).then_inc(sem["wl%d" % k], 16)
+        here = set()
+
+        def pack_x(t0, nt, name):
+            for k in sorted({xchips.index(chip[t]) for t in range(t0, t0 + nt)}):
+                if k not in here:
+                    here.add(k)
+                    g.vector.wait_ge(sem["xl%d" % k], 16)
+            p = pos[t0]
+            g.vector.quantize_mx(T.xq[:, p * TW:(p + nt) * TW], T.xs[:, p * TW:(p + nt) * TW],
+                                 T.xb[:, t0 * TB:(t0 + nt) * TB]).then_inc(sem[name], 1)
+
+        for k, sh in enumerate(ships):
+            for (t0, nt) in _runs(sh["tiles"]):
+                pack_x(t0, nt, "xd%d" % k)
+        pack_x(rank, 1, "xo")
+        for k, (t0, nt) in enumerate(wp):
+            g.vector.wait_ge(sem["wl%d" % k], 16)
+            g.vector.quantize_mx(T.wq[:, t0 * TW:(t0 + nt) * TW], T.ws[:, t0 * TW:(t0 + nt) * TW],
+                                 T.wb[:, t0 * TB:(t0 + nt) * TB]).then_inc(sem["wd%d" % k], 1)
+
+    sent = 0
+    for waits, part, trs in plan["calls"].get(core, []):
+        for name, val in waits:
+            g.wait_ge(sem[name], val)
+        lst = []
+        for (dst, sb, st, db, dtile, nt, es, name) in trs:
+            rid, pid, _se = topo.addr(dst)
+            lst.append(RemoteDMATransfer(dst_ids=[DstId(rid=rid, pnc=pid)], dma_engine_mask=_mask(es),
+                                         remote_sem=sem[name], src=view(part, sb, st, nt),
+                                         dst=view(part, db, dtile, nt)))
+            sent += len(es)
+        g.remote_dma_fused(lst, local_sem=sem.sent)
+    if rank is not None and W_FREE < len(plan["wp"][rank]):
+        g.sem_inc(sem.gate, 1)
+    if sent:
+        g.wait_ge(sem.sent, sent)
+    if rank is None:
+        return
+
+    order = plan["mm"][rank]
+    seen = set()
+    last = None
+    for i, j in enumerate(order):
+        k = [k for k, (t0, nt) in enumerate(wp) if t0 <= j < t0 + nt][0]
+        if k not in seen:
+            seen.add(k)
+            g.tensor.wait_ge(sem["wd%d" % k], 1)
+        if j == rank:
+            g.tensor.wait_ge(sem.xo, 1)
+            rq, rs, p = T.xq, T.xs, pos[rank]
+        else:
+            g.tensor.wait_ge(sem["a%d" % j], plan["arrive"][(j, rank)])
+            rq, rs, p = T.lq, T.ls, j
+        last = g.tensor.matmul_mx(T.acc[:, 0:TW], T.wq[:, j * TW:(j + 1) * TW], T.ws[:, j * TW:(j + 1) * TW],
+                                  rq[:, p * TW:(p + 1) * TW], rs[:, p * TW:(p + 1) * TW], i == 0, i == len(order) - 1)
+    last.then_inc(sem.mm, 1)
+    g.vector.wait_ge(sem.mm, 1)
+    g.vector.tensor_copy(T.yo[:], T.acc[:, 0:TW]).then_inc(sem.cp, 1)
+    g.sync.wait_ge(sem.cp, 1)
+    g.sync.dma_start(T.y[:], T.yo[:]).then_inc(sem.st, 16)
+    g.sync.wait_ge(sem.st, 16)

@@ -7,10 +7,6 @@ TW = 128
 TB = 4 * TW
 RELAY_TILES = 6
 W_FREE = 1
-HAND = False
-NEEDY_FIRST = True
-ABROAD = True
-PAIR = "direct"
 
 SCRATCH = {
     "xb": ("sbuf", [128, N * TB], "bfloat16"),
@@ -73,49 +69,68 @@ def _plan(cores, topo):
     for r in range(n):
         group.setdefault(chip[r], []).append(r)
     free = [c for c in range(SIM_CORES) if c not in cores]
+    chips = sorted({topo.chip(c) for c in range(SIM_CORES)})
 
     def ok(c, rs):
         return all(topo.may_write(c, cores[r]) for r in rs)
 
-    def hops(ca, cb):
-        return 0 if ca == cb else 1 if topo.mates(ca, cb) or topo.same_plane(ca, cb) else 2
+    def way(c, cb):
+        ca, d = topo.chip(c), topo.die(c)
+        if ca == cb:
+            return []
+        if topo.mates(ca, cb):
+            return [("mate", ca, d)]
+        if topo.same_plane(ca, cb):
+            return [("out", ca, d), ("in", cb, d)]
+        m = [x for x in chips if topo.mates(ca, x)][0]
+        return [("mate", ca, d), ("out", m, d), ("in", cb, d)]
 
-    busy = {}
+    load, busy = {}, {}
 
-    def pick(s, cb):
-        cand = [c for c in free if topo.may_write(s, c) and ok(c, group[cb])]
-        h = min(cand, key=lambda c: (busy.get(c, 0), hops(topo.chip(s), topo.chip(c)) + hops(topo.chip(c), cb),
-                                     topo.chip(c) != topo.chip(s), topo.die(c) != topo.die(s),
-                                     sum(topo.may_write(c, o) for o in cores), c))
-        busy[h] = busy.get(h, 0) + 1
-        return h
+    def put(c, cb, k):
+        for l in way(c, cb):
+            load[l] = load.get(l, 0) + k
 
     reach = {j: [cb for cb in sorted(group) if cb != chip[j] and ok(cores[j], group[cb])] for j in range(n)}
+    for j in range(n):
+        for cb in reach[j]:
+            put(cores[j], cb, len(group[cb]))
     ships = {}
-    for j in sorted(range(n), key=lambda j: (len(reach[j]) if NEEDY_FIRST or reach[j] else n, j)):
+    for j in sorted(range(n), key=lambda j: (len(reach[j]), j)):
         s = cores[j]
         away = [cb for cb in sorted(group) if cb != chip[j]]
-        handed = [cb for cb in away if cb not in reach[j]]
-        if HAND and not handed:
-            idle = {cb: [c for c in free if topo.may_write(s, c) and not busy.get(c) and ok(c, group[cb])
-                         and (ABROAD or topo.chip(c) == chip[j])] for cb in away}
-            way = {cb: min([(hops(chip[j], topo.chip(c)) + hops(topo.chip(c), cb)) for c in idle[cb]] + [n])
-                   for cb in away}
-            best = min(away, key=lambda cb: (way[cb], -len(idle[cb])))
-            if idle[best]:
-                handed = [best]
+        must = [cb for cb in away if cb not in reach[j]]
         mine = []
-        for cb in sorted(handed, key=lambda cb: -hops(chip[j], cb)):
-            mine.append({"tiles": list(group[cb]), "via": pick(s, cb)})
-        pair = [r for r in group[chip[j]] if r != j]
-        near = [sh for sh in mine if topo.chip(sh["via"]) == chip[j]]
-        if PAIR == "joined" and near:
-            near[-1]["tiles"] += pair
-            pair = []
-        for cb in sorted([cb for cb in away if cb not in handed], key=lambda cb: -hops(chip[j], cb)):
+        for opts in ([[cb] for cb in must] or [away]):
+            best = None
+            for cb in opts:
+                k = len(group[cb])
+                for h in free:
+                    if (busy.get(h) and not must) or topo.chip(h) != chip[j] or not topo.may_write(s, h) or not ok(h, group[cb]):
+                        continue
+                    if cb in reach[j]:
+                        put(s, cb, -k)
+                    put(h, cb, k)
+                    score = (busy.get(h, 0), max(load.values()), sum(v * v for v in load.values()),
+                             topo.die(h) != topo.die(s), sum(topo.may_write(h, o) for o in cores), h)
+                    put(h, cb, -k)
+                    if cb in reach[j]:
+                        put(s, cb, k)
+                    if best is None or score < best[0]:
+                        best = (score, cb, h)
+            if best is None:
+                continue
+            cb, h = best[1], best[2]
+            if cb in reach[j]:
+                put(s, cb, -len(group[cb]))
+            put(h, cb, len(group[cb]))
+            busy[h] = busy.get(h, 0) + 1
+            mine.append({"tiles": list(group[cb]), "via": h})
+        handed = [chip[sh["tiles"][0]] for sh in mine]
+        mine.sort(key=lambda sh: -len(way(sh["via"], chip[sh["tiles"][0]])))
+        for cb in sorted([cb for cb in away if cb not in handed], key=lambda cb: -len(way(s, cb))):
             mine.append({"tiles": list(group[cb]), "via": None})
-        if pair:
-            mine.append({"tiles": pair, "via": near[-1]["via"] if PAIR == "helper" and near else None})
+        mine.append({"tiles": [r for r in group[chip[j]] if r != j], "via": None})
         ships[j] = mine
 
     pos = {}
@@ -123,7 +138,7 @@ def _plan(cores, topo):
         seq = [r for sh in ships[j] for r in sh["tiles"]] + [j]
         pos[j] = {r: i for i, r in enumerate(seq)}
 
-    calls, arrive, turn, slots, tasks, took = {}, {}, {}, {}, {}, {}
+    calls, arrive, turn, slots, tasks = {}, {}, {}, {}, {}
 
     def lanes(c):
         far = _bits(topo.mask(c, [o for o in cores if topo.chip(o) != topo.chip(c)][0]))
@@ -131,47 +146,53 @@ def _plan(cores, topo):
                 if e not in far]
         return far, near
 
-    def fan_out(c, waits, buf, where, j, tiles):
+    def fan_out(c, waits, parts, buf, where, j, tiles):
         far, near = lanes(c)
         out = [r for r in tiles if chip[r] != topo.chip(c)]
         stay = [r for r in tiles if chip[r] == topo.chip(c)]
-        for part in ("c", "s"):
+        for part in parts:
             t = turn.get(c, 0)
             share = dict(zip(out, _split(far, len(out), t % 4 in (1, 2)))) if out else {}
             if out:
                 turn[c] = t + 1
             if stay:
-                share.update(zip(stay, _split(near, len(stay), False)))
+                share.update(zip(stay, _split(near if out else far + near, len(stay), False)))
             trs = []
             for r in tiles:
                 trs.append((cores[r], buf, where[r], "l", j, 1, share[r], "a%d" % j))
                 arrive[(j, r)] = arrive.get((j, r), 0) + len(share[r])
             calls.setdefault(c, []).append((waits[part], part, trs))
 
-    for k in range(max(len(s) for s in ships.values())):
-        for j in range(n):
-            if k >= len(ships[j]):
-                continue
-            sh, s = ships[j][k], cores[j]
-            ready = [("xd%d" % k, len(_runs(sh["tiles"])))]
-            if sh["via"] is None:
-                fan_out(s, {"c": ready, "s": []}, "x", pos[j], j, sh["tiles"])
-                continue
+    late, todo = {}, []
+    for j in sorted(range(n), key=lambda j: (sum(sh["via"] is not None for sh in ships[j]), j)):
+        s = cores[j]
+        far, near = lanes(s)
+        hand = [(k, sh) for k, sh in enumerate(ships[j]) if sh["via"] is not None]
+        es = [near] if len(hand) == 1 else [far, near]
+        place = []
+        for i, (k, sh) in enumerate(hand):
             h = sh["via"]
-            far, near = lanes(s)
-            es = far
-            if topo.chip(h) == chip[j]:
-                must = sum(1 for o in ships[j] if (o["via"] is None and chip[o["tiles"][0]] != chip[j])
-                           or (o["via"] is not None and topo.chip(o["via"]) != chip[j]))
-                es = near if must or took.get(s) else far
-                took[s] = True
             slot, t = slots.get(h, 0), tasks.get(h, 0)
             slots[h], tasks[h] = slot + len(sh["tiles"]), t + 1
-            for part in ("c", "s"):
-                calls.setdefault(s, []).append((ready if part == "c" else [], part, [
-                    (h, "x", pos[j][sh["tiles"][0]], "r", slot, len(sh["tiles"]), es, "b%s%d" % (part, t))]))
-            fan_out(h, {"c": [("bc%d" % t, len(es))], "s": [("bs%d" % t, len(es))]}, "r",
-                    {r: slot + i for i, r in enumerate(sh["tiles"])}, j, sh["tiles"])
+            place.append((slot, t))
+            late[(j, k)] = t + 0.5 * i
+        trs = {part: [(sh["via"], "x", pos[j][sh["tiles"][0]], "r", place[i][0], len(sh["tiles"]), es[i],
+                       "b%s%d" % (part, place[i][1])) for i, (k, sh) in enumerate(hand)] for part in ("s", "c")}
+        for i, (k, sh) in enumerate(hand):
+            calls.setdefault(s, []).append(([("xd%d" % k, len(_runs(sh["tiles"])))], "s", [trs["s"][i]]))
+        if hand:
+            calls[s].append(([], "c", trs["c"]))
+        rest = [(k, sh) for k, sh in enumerate(ships[j]) if sh["via"] is None]
+        if len(rest) > 2:
+            k, sh = rest.pop(0)
+            fan_out(s, {"c": [("xd%d" % k, len(_runs(sh["tiles"])))], "s": []}, ("c", "s"), "x", pos[j], j, sh["tiles"])
+        fan_out(s, {"c": [("xd%d" % k, len(_runs(sh["tiles"]))) for k, sh in rest], "s": []}, ("c", "s"), "x", pos[j], j,
+                [r for k, sh in rest for r in sh["tiles"]])
+        todo += [(sh["via"], place[i], len(es[i]), j, sh["tiles"]) for i, (k, sh) in enumerate(hand)]
+    own = {c: len(v) for c, v in calls.items()}
+    for h, (slot, t), ne, j, tiles in todo:
+        fan_out(h, {"c": [("bc%d" % t, ne)], "s": [("bs%d" % t, ne)]},
+                ("s", "c"), "r", {r: slot + q for q, r in enumerate(tiles)}, j, tiles)
 
     mm, wp = {}, {}
     for r in range(n):
@@ -179,7 +200,7 @@ def _plan(cores, topo):
         for j in range(n):
             for k, sh in enumerate(ships[j]):
                 if r in sh["tiles"]:
-                    eta[j] = k + 1.5 * (sh["via"] is not None)
+                    eta[j] = (2.0 + late[(j, k)] if sh["via"] is not None else 1.0) + 0.1 * len(way(cores[j], chip[r]))
         chips_in = sorted(group, key=lambda cb: max(eta[j] for j in group[cb]))
         parts = []
         for i, cb in enumerate(chips_in):
@@ -192,7 +213,7 @@ def _plan(cores, topo):
                 order += [j for j in js if t0 <= j < t0 + nt]
         mm[r], wp[r] = order, wparts
     return {"ships": ships, "pos": pos, "calls": calls, "arrive": arrive, "mm": mm, "wp": wp, "group": group,
-            "chip": chip}
+            "chip": chip, "own": own}
 
 
 def rank_program(g, core, T, topo):
@@ -245,7 +266,7 @@ def rank_program(g, core, T, topo):
                                  T.wb[:, t0 * TB:(t0 + nt) * TB]).then_inc(sem["wd%d" % k], 1)
 
     sent = 0
-    for waits, part, trs in plan["calls"].get(core, []):
+    for i, (waits, part, trs) in enumerate(plan["calls"].get(core, [])):
         for name, val in waits:
             g.wait_ge(sem[name], val)
         lst = []
@@ -256,8 +277,8 @@ def rank_program(g, core, T, topo):
                                          dst=view(part, db, dtile, nt)))
             sent += len(es)
         g.remote_dma_fused(lst, local_sem=sem.sent)
-    if rank is not None and W_FREE < len(plan["wp"][rank]):
-        g.sem_inc(sem.gate, 1)
+        if rank is not None and i == plan["own"][core] - 1 and W_FREE < len(plan["wp"][rank]):
+            g.sem_inc(sem.gate, 1)
     if sent:
         g.wait_ge(sem.sent, sent)
     if rank is None:

from concourse.bass import DstId, RemoteDMATransfer
from concourse.mybir import dt

N = 9
SIM_CORES = 32
TW = 128
TB = 4 * TW
RELAY_TILES = 6
W_FREE = 1

SCRATCH = {
    "xb": ("sbuf", [128, N * TB], "bfloat16"),
    "wb": ("sbuf", [128, N * TB], "bfloat16"),
    "xq": ("sbuf", [128, N * TW], "float8_e4m3fn_x4"),
    "xs": ("sbuf", [128, N * TW], "uint8"),
    "wq": ("sbuf", [128, N * TW], "float8_e4m3fn_x4"),
    "ws": ("sbuf", [128, N * TW], "uint8"),
    "lq": ("sbuf", [128, N * TW], "float8_e4m3fn_x4"),
    "ls": ("sbuf", [128, N * TW], "uint8"),
    "rq": ("sbuf", [128, RELAY_TILES * TW], "float8_e4m3fn_x4"),
    "rs": ("sbuf", [128, RELAY_TILES * TW], "uint8"),
    "acc": ("psum", [128, 512], "float32"),
    "yo": ("sbuf", [128, TW], "float32"),
}
SEMAPHORES = (["xl%d" % k for k in range(3)] + ["xd%d" % k for k in range(4)] + ["xo"]
              + ["wl%d" % k for k in range(5)] + ["wd%d" % k for k in range(5)]
              + ["a%d" % j for j in range(N)]
              + ["bc%d" % k for k in range(3)] + ["bs%d" % k for k in range(3)]
              + ["sent", "gate", "mm", "cp", "st"])


def _bits(m):
    return [e for e in range(m.bit_length()) if (m >> e) & 1]


def _mask(es):
    m = 0
    for e in es:
        m |= 1 << e
    return m


def _split(es, k, flip):
    h = len(es) // 2
    q = h // 2
    if k == 1:
        return [es]
    if k == 2:
        return [es[:h], es[h:]]
    if flip:
        return [es[:q], es[q:h], es[h:]]
    return [es[:h], es[h:h + q], es[h + q:]]


def _runs(ts):
    out = []
    for t in ts:
        if out and out[-1][0] + out[-1][1] == t:
            out[-1] = (out[-1][0], out[-1][1] + 1)
        else:
            out.append((t, 1))
    return out


def _plan(cores, topo):
    n = len(cores)
    chip = [topo.chip(c) for c in cores]
    group = {}
    for r in range(n):
        group.setdefault(chip[r], []).append(r)
    free = [c for c in range(SIM_CORES) if c not in cores]
    chips = sorted({topo.chip(c) for c in range(SIM_CORES)})

    def ok(c, rs):
        return all(topo.may_write(c, cores[r]) for r in rs)

    def way(c, cb):
        ca, d = topo.chip(c), topo.die(c)
        if ca == cb:
            return []
        if topo.mates(ca, cb):
            return [("mate", ca, d)]
        if topo.same_plane(ca, cb):
            return [("out", ca, d), ("in", cb, d)]
        m = [x for x in chips if topo.mates(ca, x)][0]
        return [("mate", ca, d), ("out", m, d), ("in", cb, d)]

    load, busy = {}, {}

    def put(c, cb, k):
        for l in way(c, cb):
            load[l] = load.get(l, 0) + k

    reach = {j: [cb for cb in sorted(group) if cb != chip[j] and ok(cores[j], group[cb])] for j in range(n)}
    for j in range(n):
        for cb in reach[j]:
            put(cores[j], cb, len(group[cb]))
    ships = {}
    for j in sorted(range(n), key=lambda j: (len(reach[j]), j)):
        s = cores[j]
        away = [cb for cb in sorted(group) if cb != chip[j]]
        must = [cb for cb in away if cb not in reach[j]]
        mine = []
        for opts in ([[cb] for cb in must] or [away]):
            best = None
            for cb in opts:
                k = len(group[cb])
                for h in free:
                    if (busy.get(h) and not must) or topo.chip(h) != chip[j] or not topo.may_write(s, h) or not ok(h, group[cb]):
                        continue
                    if cb in reach[j]:
                        put(s, cb, -k)
                    put(h, cb, k)
                    score = (busy.get(h, 0), max(load.values()), sum(v * v for v in load.values()),
                             topo.die(h) != topo.die(s), sum(topo.may_write(h, o) for o in cores), h)
                    put(h, cb, -k)
                    if cb in reach[j]:
                        put(s, cb, k)
                    if best is None or score < best[0]:
                        best = (score, cb, h)
            if best is None:
                continue
            cb, h = best[1], best[2]
            if cb in reach[j]:
                put(s, cb, -len(group[cb]))
            put(h, cb, len(group[cb]))
            busy[h] = busy.get(h, 0) + 1
            mine.append({"tiles": list(group[cb]), "via": h})
        handed = [chip[sh["tiles"][0]] for sh in mine]
        mine.sort(key=lambda sh: -len(way(sh["via"], chip[sh["tiles"][0]])))
        for cb in sorted([cb for cb in away if cb not in handed], key=lambda cb: -len(way(s, cb))):
            mine.append({"tiles": list(group[cb]), "via": None})
        mine.append({"tiles": [r for r in group[chip[j]] if r != j], "via": None})
        ships[j] = mine

    pos = {}
    for j in range(n):
        seq = [r for sh in ships[j] for r in sh["tiles"]] + [j]
        pos[j] = {r: i for i, r in enumerate(seq)}

    calls, arrive, turn, slots, tasks = {}, {}, {}, {}, {}

    def lanes(c):
        far = _bits(topo.mask(c, [o for o in cores if topo.chip(o) != topo.chip(c)][0]))
        near = [e for e in _bits(topo.mask(c, [o for o in range(SIM_CORES) if topo.chip(o) == topo.chip(c) and o != c][0]))
                if e not in far]
        return far, near

    def fan_out(c, waits, parts, buf, where, j, tiles):
        far, near = lanes(c)
        out = [r for r in tiles if chip[r] != topo.chip(c)]
        stay = [r for r in tiles if chip[r] == topo.chip(c)]
        for part in parts:
            t = turn.get(c, 0)
            share = dict(zip(out, _split(far, len(out), t % 4 in (1, 2)))) if out else {}
            if out:
                turn[c] = t + 1
            if stay:
                share.update(zip(stay, _split(near if out else far + near, len(stay), False)))
            trs = []
            for r in tiles:
                trs.append((cores[r], buf, where[r], "l", j, 1, share[r], "a%d" % j))
                arrive[(j, r)] = arrive.get((j, r), 0) + len(share[r])
            calls.setdefault(c, []).append((waits[part], part, trs))

    late, todo = {}, []
    for j in sorted(range(n), key=lambda j: (sum(sh["via"] is not None for sh in ships[j]), j)):
        s = cores[j]
        far, near = lanes(s)
        hand = [(k, sh) for k, sh in enumerate(ships[j]) if sh["via"] is not None]
        es = [near] if len(hand) == 1 else [far, near]
        place = []
        for i, (k, sh) in enumerate(hand):
            h = sh["via"]
            slot, t = slots.get(h, 0), tasks.get(h, 0)
            slots[h], tasks[h] = slot + len(sh["tiles"]), t + 1
            place.append((slot, t))
            late[(j, k)] = t + 0.5 * i
        trs = {part: [(sh["via"], "x", pos[j][sh["tiles"][0]], "r", place[i][0], len(sh["tiles"]), es[i],
                       "b%s%d" % (part, place[i][1])) for i, (k, sh) in enumerate(hand)] for part in ("s", "c")}
        for i, (k, sh) in enumerate(hand):
            calls.setdefault(s, []).append(([("xd%d" % k, len(_runs(sh["tiles"])))], "s", [trs["s"][i]]))
        if hand:
            calls[s].append(([], "c", trs["c"]))
        rest = [(k, sh) for k, sh in enumerate(ships[j]) if sh["via"] is None]
        if len(rest) > 2:
            k, sh = rest.pop(0)
            fan_out(s, {"c": [("xd%d" % k, len(_runs(sh["tiles"])))], "s": []}, ("c", "s"), "x", pos[j], j, sh["tiles"])
        fan_out(s, {"c": [("xd%d" % k, len(_runs(sh["tiles"]))) for k, sh in rest], "s": []}, ("c", "s"), "x", pos[j], j,
                [r for k, sh in rest for r in sh["tiles"]])
        todo += [(sh["via"], place[i], len(es[i]), j, sh["tiles"]) for i, (k, sh) in enumerate(hand)]
    own = {c: len(v) for c, v in calls.items()}
    for h, (slot, t), ne, j, tiles in todo:
        fan_out(h, {"c": [("bc%d" % t, ne)], "s": [("bs%d" % t, ne)]},
                ("s", "c"), "r", {r: slot + q for q, r in enumerate(tiles)}, j, tiles)

    mm, wp = {}, {}
    for r in range(n):
        eta = {r: -1.0}
        for j in range(n):
            for k, sh in enumerate(ships[j]):
                if r in sh["tiles"]:
                    eta[j] = (2.0 + late[(j, k)] if sh["via"] is not None else 1.0) + 0.1 * len(way(cores[j], chip[r]))
        chips_in = sorted(group, key=lambda cb: max(eta[j] for j in group[cb]))
        parts = []
        for i, cb in enumerate(chips_in):
            js = sorted(group[cb], key=lambda j: eta[j])
            parts += [js[:-1], js[-1:]] if i == len(chips_in) - 1 else [js]
        order, wparts = [], []
        for js in parts:
            for (t0, nt) in _runs(sorted(js)):
                wparts.append((t0, nt))
                order += [j for j in js if t0 <= j < t0 + nt]
        mm[r], wp[r] = order, wparts
    return {"ships": ships, "pos": pos, "calls": calls, "arrive": arrive, "mm": mm, "wp": wp, "group": group,
            "chip": chip, "own": own}


def rank_program(g, core, T, topo):
    cores = list(T.cores)
    plan = _plan(cores, topo)
    sem = T.sem
    rank = T.rank_of(core)
    codes = {"x": T.xq, "r": T.rq, "l": T.lq}
    planes = {"x": T.xs, "r": T.rs, "l": T.ls}

    def view(part, buf, tile, nt):
        if part == "c":
            return codes[buf][:, tile * TW:(tile + nt) * TW].bitcast(dt.uint8)
        return planes[buf][:, tile * TW:(tile + nt) * TW]

    if rank is not None:
        ships, pos, group, chip = plan["ships"][rank], plan["pos"][rank], plan["group"], plan["chip"]
        xchips = []
        for r in [r for sh in ships for r in sh["tiles"]] + [rank]:
            if chip[r] not in xchips:
                xchips.append(chip[r])
        for k, cb in enumerate(xchips):
            a, b = group[cb][0] * TB, (group[cb][-1] + 1) * TB
            q = g.sync if k % 2 == 0 else g.scalar
            q.dma_start(T.xb[:, a:b], T.x[:, a:b]).then_inc(sem["xl%d" % k], 16)
        wp = plan["wp"][rank]
        for k, (t0, nt) in enumerate(wp):
            if k == W_FREE:
                g.scalar.wait_ge(sem.gate, 1)
            g.scalar.dma_start(T.wb[:, t0 * TB:(t0 + nt) * TB],
                               T.w[:, t0 * TB:(t0 + nt) * TB]).then_inc(sem["wl%d" % k], 16)
        here = set()

        def pack_x(t0, nt, name):
            for k in sorted({xchips.index(chip[t]) for t in range(t0, t0 + nt)}):
                if k not in here:
                    here.add(k)
                    g.vector.wait_ge(sem["xl%d" % k], 16)
            p = pos[t0]
            g.vector.quantize_mx(T.xq[:, p * TW:(p + nt) * TW], T.xs[:, p * TW:(p + nt) * TW],
                                 T.xb[:, t0 * TB:(t0 + nt) * TB]).then_inc(sem[name], 1)

        for k, sh in enumerate(ships):
            for (t0, nt) in _runs(sh["tiles"]):
                pack_x(t0, nt, "xd%d" % k)
        pack_x(rank, 1, "xo")
        for k, (t0, nt) in enumerate(wp):
            g.vector.wait_ge(sem["wl%d" % k], 16)
            g.vector.quantize_mx(T.wq[:, t0 * TW:(t0 + nt) * TW], T.ws[:, t0 * TW:(t0 + nt) * TW],
                                 T.wb[:, t0 * TB:(t0 + nt) * TB]).then_inc(sem["wd%d" % k], 1)

    sent = 0
    for i, (waits, part, trs) in enumerate(plan["calls"].get(core, [])):
        for name, val in waits:
            g.wait_ge(sem[name], val)
        lst = []
        for (dst, sb, st, db, dtile, nt, es, name) in trs:
            rid, pid, _se = topo.addr(dst)
            lst.append(RemoteDMATransfer(dst_ids=[DstId(rid=rid, pnc=pid)], dma_engine_mask=_mask(es),
                                         remote_sem=sem[name], src=view(part, sb, st, nt),
                                         dst=view(part, db, dtile, nt)))
            sent += len(es)
        g.remote_dma_fused(lst, local_sem=sem.sent)
        if rank is not None and i == plan["own"][core] - 1 and W_FREE < len(plan["wp"][rank]):
            g.sem_inc(sem.gate, 1)
    if sent:
        g.wait_ge(sem.sent, sent)
    if rank is None:
        return

    order = plan["mm"][rank]
    seen = set()
    last = None
    for i, j in enumerate(order):
        k = [k for k, (t0, nt) in enumerate(wp) if t0 <= j < t0 + nt][0]
        if k not in seen:
            seen.add(k)
            g.tensor.wait_ge(sem["wd%d" % k], 1)
        if j == rank:
            g.tensor.wait_ge(sem.xo, 1)
            rq, rs, p = T.xq, T.xs, pos[rank]
        else:
            g.tensor.wait_ge(sem["a%d" % j], plan["arrive"][(j, rank)])
            rq, rs, p = T.lq, T.ls, j
        last = g.tensor.matmul_mx(T.acc[:, 0:TW], T.wq[:, j * TW:(j + 1) * TW], T.ws[:, j * TW:(j + 1) * TW],
                                  rq[:, p * TW:(p + 1) * TW], rs[:, p * TW:(p + 1) * TW], i == 0, i == len(order) - 1)
    last.then_inc(sem.mm, 1)
    g.vector.wait_ge(sem.mm, 1)
    g.vector.tensor_copy(T.yo[:], T.acc[:, 0:TW]).then_inc(sem.cp, 1)
    g.sync.wait_ge(sem.cp, 1)
    g.sync.dma_start(T.y[:], T.yo[:]).then_inc(sem.st, 16)
    g.sync.wait_ge(sem.st, 16)
